import numpy as np, ml_dtypes
CORES = [5,29,101,125,133,157,229,253]
N = 8
import mx_ref
BF = ml_dtypes.bfloat16
def gcols(t, e):
    v = np.concatenate([t.reshape(8, 16, -1, 4), np.zeros((8, 16, 1, 4), BF)], axis=2)
    return np.ascontiguousarray(np.stack([v[g][:, e[g]] for g in range(8)])).reshape(128, -1)
def tile(rs):
    return np.stack(rs, axis=2).reshape(128, -1).astype(BF)
def pick(q, e):
    c = np.concatenate([q[0].reshape(128, -1, 4), np.zeros((128, 1, 4), np.uint8)], axis=1); s = np.concatenate([q[1], np.ones((16, 1), np.uint8)], axis=1)
    return (np.ascontiguousarray(c[:, e].reshape(128, -1)), np.ascontiguousarray(s[:, e]))
def join(*qs):
    return (np.concatenate([q[0] for q in qs], axis=1), np.concatenate([q[1] for q in qs], axis=1))
def put(q, e, v):
    c, s = q[0].reshape(128, -1, 4).copy(), q[1].copy(); c[:, e] = v[0].reshape(128, -1, 4); s[:, e] = v[1]
    return (c.reshape(128, -1), s)
def pk(c, s):
    return (np.ascontiguousarray(c), mx_ref.live(s))
def emit(q):
    return q[0], q[1]
def packed(v, rng):
    q = [mx_ref.quantize(np.ascontiguousarray(v[r])) for r in range(N)]
    return np.stack([a for a, b in q]), np.stack([mx_ref.plane(b, rng) for a, b in q])
def values_of_codes():
    e, c = np.zeros((128, 128, 4), np.float32), np.zeros((128, 2, 4), np.uint8)
    e[np.arange(128), np.arange(128), 0] = 1
    c[:127, :, 0] = np.arange(256).reshape(2, 128).T[:127]
    return mx_ref.matmul(mx_ref.quantize(e.reshape(128, 512).astype(BF)), (c.reshape(128, 8), np.full((16, 2), 127, np.uint8))).T.reshape(-1).astype(np.float64)
CODE_VALUE, SCALE_VALUE = values_of_codes(), 2.0 ** (np.arange(256) - 127.0)
def decode(q):
    return (CODE_VALUE[q[0]].reshape(16, 8, -1, 4) * SCALE_VALUE[q[1]][:, None, :, None] + 0.0).reshape(128, -1).astype(np.float32)
def f(rng, *shape):
    return mx_ref.flush((rng.standard_normal(shape, dtype=np.float32) * np.exp2(rng.integers(-2, 3, shape[:-1] + (1,)))).astype(BF))
def wide(rng, *shape, cols=0):
    v = rng.standard_normal(shape, dtype=np.float32) * np.exp2(rng.integers(-12, 13, shape)).astype(np.float32)
    if cols: v *= np.repeat(np.exp2(rng.integers(-cols, cols + 1, shape[:-2] + (1, shape[-1] // 4))) * (rng.random(shape[:-2] + (1, shape[-1] // 4)) > 0.0625), 4, axis=-1).astype(np.float32)
    return mx_ref.flush(v.astype(BF))
C, P, R = 256, 64, 2
def big(v):
    v = v.astype(np.float32)
    v[np.abs(v) < np.float32(2.0 ** -16)] = 0
    return v.astype(BF)
def numbers_of(rng):
    return {"x": big(f(rng, N, 128, 4 * C)), "u": np.array(f(rng, N, 128, 512)), "v": np.array(f(rng, N, 128, 512))}
def layers(rng):
    return big(f(rng, N, 128, 2048)).reshape(N, 8, 16, 4, 8, 16, 4)
def weights(rng, w):
    c, p = packed(np.ascontiguousarray(w).reshape(N, 128, 2048), rng)
    return {"wc": c, "ws": p}
def setup_inputs(rng):
    return {**numbers_of(rng), **weights(rng, layers(rng))}
def setup_inputs_ties(rng):
    d = numbers_of(rng)
    e = rng.permutation(N)
    x = d["x"].reshape(N, 8, 16, C, 4)
    for r in range(N):
        k = rng.permutation(C) % 3
        if r == e[0]: k = np.zeros(C, int)
        elif r in e[2::2]: k = rng.permutation(3)[np.arange(C) % 3]
        a = x[r][:, :8, :3].copy()
        a[:, :, 2] = 0
        x[r][:, :8] = a[:, :, k]
    x[e[1]] = 0
    u = d["u"].reshape(N, 8, 16, 128, 4)
    for i in range(5): u[:, :, 8:, i::16] = 0
    w = layers(rng)
    w[:, :, :, :, :, :8] = 0
    return {"x": x.reshape(N, 128, 4 * C), "u": u.reshape(N, 128, 512), "v": d["v"], **weights(rng, w)}
def setup_inputs_near(rng):
    d = numbers_of(rng)
    x = d["x"].astype(np.float32).reshape(N, 8, 16, C, 4)
    x[:, :, :9] = 0
    u = d["u"].reshape(N, 128, 128, 4)
    for i in range(5): u[:, :, i::16] = 0
    o = rng.permutation(N) % 4
    for r in range(N):
        k = 2.0 ** -30 if o[r] else 1.0
        c = rng.integers(0, 2, (8, 1)) * 2.0 - 1.0
        s = rng.integers(-1, 2, (8, C, 4))
        if o[r] < 2:
            n = rng.integers(0, 16, (8, C))
            x[r, :, 0] = ((n[:, :, None] >> np.arange(4)) & 1) * np.exp2(np.arange(4) - 23.0)
            x[r, :, 1, :, 0] = 2.0 ** -10
            x[r, :, 2] = s * 2.0 ** -10
            x[r, :, 8, :, 0] = c
        else:
            x[r, :, 0, :, 0] = c * rng.integers(1, 16, (8, C)) * 2.0 ** -29
            x[r, :, 2] = s * 2.0 ** -29
        for g in rng.permutation(8)[:4]: x[r, g, 8 if o[r] < 2 else 0, rng.integers(C), 0] = 2.0 ** 29 * (rng.integers(0, 2) * 2.0 - 1.0)
        for h in range(0, 128, 16):
            u[r, h, h + 4] = k
            u[r, h + 1, h + 4, 0] = k
            u[r, h + 8, h + 4, 0] = k
            for i in range(4): u[r, h + 2, h + i, i] = k
    w = layers(rng)
    w[:, :, :9] = 0
    w[:, :, :, :, :, :9] = 0
    return {"x": x.reshape(N, 128, 4 * C).astype(BF), "u": u.reshape(N, 128, 512), "v": d["v"], **weights(rng, w)}
def setup_inputs_skew(rng):
    d = numbers_of(rng)
    x = d["x"].astype(np.float32).reshape(N, 8, 16, C, 4)
    t = (1 + (2 * rng.integers(0, 64, (N, 8, 8, C // 2, 4)) + 1) / 128) * np.exp2(-rng.integers(8, 15, (N, 8, 8, C // 2, 4)).astype(float)) * (rng.integers(0, 2, (N, 8, 8, C // 2, 4)) * 2.0 - 1.0)
    t[:, :, 3, :, 1] = 1.96875
    x[:, :, 8:, ::2] = t * np.exp2(rng.integers(-2, 3, (N, 8, 1, C // 2, 1)).astype(float))
    u = d["u"].reshape(N, 128, 128, 4)
    for i in range(5): u[:, :, i::16] = 0
    for h in range(0, 128, 16):
        for b in range(12): u[:, h + b // 4, h + 4, b % 4] = 2.0 ** b
        for i in range(4): u[:, h + 3, h + i, i] = 1
    n = -(-C // 7)
    n2 = n - (-(C - n) // 5)
    n3 = n2 - (-(C - n2) // 3)
    down = C - 1 - np.arange(C)
    for r in range(N):
        for j, g in enumerate(rng.permutation(8)):
            a = np.append(rng.permutation(np.delete(np.arange(4), j % 4)), j % 4)
            two = np.zeros((C, 4), int)
            if j < 6:
                two[:n, a[0]] = 1
                two[n:n2, a[1]] = 1
            if j < 4: two[n2:n3, a[2]] = 1
            if j >= 6: two[-(-2 * C // 5):] = 1
            o = rng.permutation(C)
            x[r, g][:3, o] = (down[None, :, None] >> (4 * np.arange(3)[:, None, None] + np.arange(4))) & 1
            x[r, g][3, o] = np.where(two > 0, 1, -rng.integers(0, 2, (C, 4)))
    w = layers(rng)
    w[:, :, :, :, :, :4] = 0
    return {"x": x.reshape(N, 128, 4 * C).astype(BF), "u": u.reshape(N, 128, 512), "v": d["v"], **weights(rng, w)}
def setup_inputs_huge(rng):
    d = numbers_of(rng)
    o = rng.permutation(N)
    h = rng.permutation(8)
    x = -0.95 - 0.05 * rng.random((N, 8, 16, C, 4))
    x[:, h[4:]] = (0.75 + 0.1 * rng.random((N, 4, 16, C, 4))) * rng.choice([-1.0, 1.0], (N, 4, 1, C, 1))
    u = d["u"].reshape(N, 128, 128, 4)
    for i in range(5): u[:, :, i::16] = 0
    for r in range(N):
        if o[r] < N // 2: x[r] = (0.8 + 0.1 * rng.random((8, 16, C, 4))) * rng.choice([-1.0, 1.0], (1, 1, C, 1))
        for g in range(8):
            for i in range(5):
                a, n = 16 * int(rng.choice(h[4:])), 16
                if i == 4 and o[r] < N // 2: a, n = 0, 128
                u[r, a:a + n, 16 * g + i] = (2.0 ** 30 * (1 - 0.05 * rng.random((n, 4))) * rng.choice([-1.0, 1.0])).astype(np.float32).astype(BF)
    w = np.zeros((N, 128, 4, 128, 4), np.float32)
    i = np.arange(128)
    for b in range(4): w[:, i, b, i, b] = -1
    return {"x": (2.0 ** 30 * x).astype(np.float32).reshape(N, 128, 4 * C).astype(BF), "u": u.reshape(N, 128, 512), "v": d["v"], **weights(rng, w.astype(BF))}
def setup_inputs_spread(rng):
    d = setup_inputs(rng)
    d["x"] = big(wide(rng, N, 128, 4 * C, cols=6))
    return d
def check_inputs(d):
    b = []
    for k in ("x", "u", "v"):
        a = np.abs(d[k].astype(np.float32))
        if not (np.isfinite(a).all() and ((a == 0) | (a >= 2.0 ** -30) & (a <= 2.0 ** 30)).all()): b.append("a value of " + k)
    none, least, most = [emit(mx_ref.quantize(np.full((128, 16), k, np.float32).astype(BF)))[1][0, 0] for k in (0.0, 2.0 ** -30, 2.0 ** 30)]
    for r in range(N):
        if ((d["wc"][r] == 0x7F) | (d["wc"][r] == 0xFF)).any(): b.append("wc: a code that is no number")
        s = mx_ref.live(d["ws"][r])
        if ((s != none) & ((s < least) | (s > most))).any(): b.append("ws: a scale out of range")
    return b
def divide(sums):
    g = np.arange(8)
    first, end = np.zeros((4, 8), np.int64), np.full((4, 8), C)
    a, left = np.zeros(8, np.int64), np.ones((4, 8), bool)
    for m in (4, 3, 2):
        worth = sums - np.stack([sums[k, g, a] for k in range(4)])[:, :, None]
        e = np.sum(m * worth < worth[:, :, -1:], axis=2)
        e[~left] = C + 1
        k = np.argmin(e, axis=0)
        first[k, g] = a
        a = e[k, g]
        end[k, g] = a
        left[k, g] = False
    first[np.argmax(left, axis=0), g] = a
    return first, end
def reference(x, u, v, wc, ws):
    qu = [mx_ref.quantize(u[r]) for r in range(N)]
    lay = [pk(wc[r], ws[r]) for r in range(N)]
    now = [x[r] for r in range(N)]
    of = [np.arange(k * P, k * P + P) for k in range(4)]
    slot_of = np.zeros((N, 8, C), np.int64)
    for t in range(R):
        sent, best, made = [], [], []
        slot_of[:] = -1
        for r in range(N):
            s = mx_ref.matmul(qu[r], mx_ref.quantize(now[r])) + np.float32(0.0)
            o = np.argsort(-s[4::16], axis=1, kind="stable")
            worth = np.stack([1 + (np.take_along_axis(s[k::16], o, axis=1) > 0) for k in range(4)])
            first, end = divide(np.concatenate([np.zeros((4, 8, 1), np.int64), np.cumsum(worth, axis=2)], axis=2))
            slots = []
            for k in range(4):
                i = first[k][:, None] + np.arange(P)
                slots.append(np.where(i < end[k][:, None], np.take_along_axis(o, np.minimum(i, C - 1), axis=1), -1))
            slots = np.concatenate(slots, axis=1)
            for g in range(8):
                j = np.nonzero(slots[g] >= 0)[0]
                slot_of[r, g, slots[g, j]] = j
            sent.append(mx_ref.quantize(gcols(now[r], slots)))
            best.append(gcols(now[r], o[:, :P]))
        for r in range(N):
            came = decode(join(*[pick(sent[(r - k) % N], of[k]) for k in range(4)]))
            z = mx_ref.quantize(((came + np.tile(best[r].astype(np.float32), (1, 4))) * np.float32(0.5)).astype(BF))
            made.append(mx_ref.quantize(tile([mx_ref.matmul(pick(lay[r], np.arange(128 * b, 128 * b + 128)), z) * np.float32(0.03125) for b in range(4)])))
        for r in range(N):
            back = decode(join(*[pick(made[(r + k) % N], of[k]) for k in range(4)])).astype(BF)
            now[r] = (now[r].astype(np.float32) + gcols(back, slot_of[r]).astype(np.float32)).astype(BF)
    y, sl = np.zeros((N, 128, C), np.float32), np.zeros((N, 8, C), np.float32)
    oc, osc = np.zeros((N, 128, 4 * C), np.uint8), np.zeros((N, 16, C), np.uint8)
    for r in range(N):
        q = mx_ref.quantize(now[r])
        y[r] = mx_ref.matmul(mx_ref.quantize(v[r]), q)
        sl[r] = slot_of[r]
        oc[r], osc[r] = emit(q)
    return {"y": y, "sl": sl, "oc": oc, "osc": osc}

@@ -1,0 +1,513 @@
+from concourse.bass import DstId, RemoteDMATransfer
+from concourse.mybir import dt, AluOpType as A, AxisListType, ActivationFunctionType as F
+
+N = 8
+BIG = float(2.0 ** 90)
+PT = 320
+PD = 272
+WD = (128, 128, 192, 256)
+SCRATCH = {}
+PLACE = {}
+PSUM = ("pr", "pd")
+
+
+def _decl():
+    f, b, i, h, q, s = "float32", "bfloat16", "int32", "uint16", "float8_e4m3fn_x4", "uint8"
+
+    def add(names, n, d, where="sbuf"):
+        for k in names.split():
+            SCRATCH[k] = (where, [128, n], d)
+            PLACE[k] = (k, 0, n)
+
+    def share(buf, d, *groups):
+        at = 0
+        for names, n in groups:
+            for k in names.split():
+                PLACE[k] = (buf, at, n)
+                at += -(-n // 32) * 32
+        SCRATCH[buf] = ("sbuf", [128, at], d)
+    add("pr pd", 2048, f, "psum")
+    add("ub vb", 512, b)
+    add("qu qv", 128, q), add("su sv", 128, s)
+    add("qu2", 256, q), add("su2", 256, s)
+    add("wq", 512, q), add("wsc", 512, s)
+    share("ci", i, ("iD dl", 256), ("iC", 512), ("iL", 8), ("iP pq pc pg", 2), ("iS", 16))
+    share("cfl", f, ("fI maskb d0 ones io20 kk01 bigt", 256), ("ek", 2056), ("tb", 264), ("cf ch ca1 ca2 ca3 kf kc0 pgf gpf", 2), ("s16p c16 k16", 16))
+    add("ul", 16, h)
+    add("gt", 512, b), add("hf ex", 516, b)
+    share("qk", q, ("qg qe0 qe1 qe2 qe3", 128)), share("sk", s, ("sg se0 se1 se2 se3", 128))
+    for k in range(4):
+        add("cm%d" % k, 4 * WD[k], b)
+    add("cme", 1024, b)
+    share("qc", q, ("qc0 qc1", 128), ("qc2", 192), ("qc3 qce", 256)), share("sc", s, ("sc0 sc1", 128), ("sc2", 192), ("sc3 sce", 256))
+    add("dd ow sg1 sg2 pay dw2 ow2 win cum dw3 ow3 ycp slr", 256, f), add("junk", 1920, b), add("junk2", 768, b)
+    share("sm", f, ("rs rt rk ck1 ck2 ck3 bs2 bs3 bt io w1 w2 w3 xa xb xc t1 t2 t3 en vl plf c1 c2 c3 z1 z2 z3 y1 y2 y3 sv1 rl sf", 16),
+          ("tm ac1 ac2 ac3 km1 km2 km3 kx1 kx2 kcb kcc fr1 fr2 fr3 dda em af1 af2 af3 cb1 cb2 cb3 cb4 db2 db3 db4 da2 da3 e1 e2", 2))
+    share("li", h, ("ro pl so ol", 16), ("ky1 ky2 ky3 ao1 ao2 ao3", 2))
+    add("xp", 1024, b), add("xs", 4 * PT, b), add("e2x", 512, b), add("dwn", 4 * PD, b)
+    add("b13 b02 za zb ha hb", 512, b), add("qza qzb", 128, q), add("sza szb", 128, s)
+    for t in range(3):
+        add("xi%d" % t, 1024, b), add("qx%d" % t, 256, q), add("sx%d" % t, 256, s)
+    for t in range(2):
+        add("qb%d lbc%d lhc%d qh%d" % ((t,) * 4), 128, q)
+        add("sb%d lbs%d lhs%d sh%d" % ((t,) * 4), 128, s)
+        add("wbc%d whc%d" % (t, t), 192, q), add("wbs%d whs%d" % (t, t), 192, s)
+        add("rbc%d rhc%d" % (t, t), 64, q), add("rbs%d rhs%d" % (t, t), 64, s)
+
+
+_decl()
+SEMAPHORES = ["ev", "es", "et", "eg", "loc"] + ["d%d" % k for k in range(14)] + [
+    "%s%s%d" % (a, b, t) for a in ("rc", "rs", "ao", "ad") for b in "bh" for t in range(2)]
+
+
+def _relays(topo, cores, r):
+    c = cores[r]
+    own = [d for d in topo.cores_of(c) if d != c and topo.may_write(d, cores[(r + 1) % N]) and topo.may_write(d, cores[(r + 3) % N])]
+    return [[d for d in own if topo.die(d) == topo.die(c)][0], [d for d in own if topo.die(d) != topo.die(c)][0]]
+
+
+def _mask(engines):
+    return sum(1 << int(e) for e in engines)
+
+
+def _relay(g, core, T, topo, r, i):
+    n = 0
+    for t in range(2):
+        for ph in "bh":
+            k = 2 * i + 1
+            dst = T.cores[(r + (k if ph == "b" else -k)) % N]
+            rid, pid = topo.addr(dst, core)
+            en = topo.engines(core, dst)
+            for w in "cs":
+                g.wait_ge(T.sem["r%s%s%d" % (w, ph, t)], 8)
+                src, d = T["r%s%s%d" % (ph, w, t)][:, 0:64], T["l%s%s%d" % (ph, w, t)][:, 64 * i:64 * i + 64]
+                if w == "c":
+                    src, d = src.bitcast(dt.uint8), d.bitcast(dt.uint8)
+                g.remote_dma(out_ap=d, in_ap=src, remote_sem=T.sem["ao%s%d" % (ph, t)], local_sem=T.sem.loc, pid=pid, routing_id=rid,
+                             dma_engine_mask=_mask(en))
+                n += len(en)
+    g.wait_ge(T.sem.loc, n)
+
+
+def rank_program(g, core, T, topo):
+    rank = T.rank_of(core)
+    if rank is None:
+        for r in range(N):
+            if core in topo.cores_of(T.cores[r]):
+                rel = _relays(topo, T.cores, r)
+                if core in rel:
+                    _relay(g, core, T, topo, r, rel.index(core))
+        return
+    eng = {"v": g.vector, "s": g.scalar, "t": g.tensor, "g": g, "y": g.sync}
+    seen = {q: {} for q in eng}
+    tot, snap, acc, nd = {}, {}, {}, [0]
+
+    def R(n, lo=0, hi=None, st=1):
+        buf, at, w = PLACE[n]
+        return (buf, at + lo, at + (w if hi is None else hi), st)
+
+    def ap(r):
+        n, lo, hi, st = r
+        return T[n][:, lo:hi] if st == 1 else T[n][:, lo:hi:st]
+
+    def meet(a, b):
+        if a[0] in PSUM:
+            return a[1] // 512 <= (b[2] - 1) // 512 and b[1] // 512 <= (a[2] - 1) // 512
+        if a[1] >= b[2] or b[1] >= a[2]:
+            return False
+        return not (a[3] == b[3] and a[3] > 1 and (a[1] - b[1]) % a[3])
+
+    def wait(q, sem, val):
+        if seen[q].get(sem, 0) >= val:
+            return
+        eng[q].wait_ge(T.sem[sem], val)
+        seen[q][sem] = val
+        for k, v in snap.get((sem, val), {}).items():
+            seen[q][k] = max(seen[q].get(k, 0), v)
+
+    def before(q, outs, ins, own, open_=False):
+        need = {}
+        for r, wr in [(r, True) for r in outs] + [(r, False) for r in ins]:
+            for o, ow, sem, val, oq in acc.get(r[0], ()):
+                if not (wr or ow or (r[0] in PSUM and oq != own)) or not meet(r, o):
+                    continue
+                if oq == own == "t" and open_:
+                    continue
+                need[sem] = max(need.get(sem, 0), val)
+        for sem in sorted(need):
+            wait(q, sem, need[sem])
+
+    def after(q, outs, ins, sem, val, own):
+        snap[(sem, val)] = dict(seen[q])
+        for r in outs:
+            l = acc.setdefault(r[0], [])
+            if r[3] == 1 and r[0] not in PSUM:
+                l[:] = [e for e in l if not (e[0][1] >= r[1] and e[0][2] <= r[2])]
+            l.append((r, True, sem, val, own))
+        for r in ins:
+            acc.setdefault(r[0], []).append((r, False, sem, val, own))
+
+    def op(q, outs, ins, call, open_=False):
+        before(q, outs, ins, q, open_)
+        sem = "e" + q
+        tot[sem] = tot.get(sem, 0) + 1
+        call(eng[q]).then_inc(T.sem[sem], 1)
+        after(q, outs, ins, sem, tot[sem], q)
+
+    def dma(q, out, in_, outs=(), ins=()):
+        before(q, outs, ins, "dma")
+        sem = "d%d" % nd[0]
+        nd[0] += 1
+        tot[sem] = 16
+        eng[q].dma_start(out, in_).then_inc(T.sem[sem], 16)
+        after(q, outs, ins, sem, 16, "dma")
+
+    def lands(sem, val, regions):
+        tot[sem] = val
+        after("g", regions, (), sem, val, "remote")
+        snap[(sem, val)] = {}
+
+    def ts(out, i, s1, op0, s2=None, op1=None, off=None):
+        cols = [s for s in (s1, s2) if isinstance(s, tuple)]
+        a1 = ap(s1) if isinstance(s1, tuple) else s1
+        a2 = ap(s2) if isinstance(s2, tuple) else s2
+        src = ap(i) if off is None else ap(i).indirect(ap(off))
+        kw = {} if op1 is None else {"op1": op1}
+        op("v", [out], [i] + cols + ([off] if off else []),
+           lambda e: e.tensor_scalar(out=ap(out), in0=src, scalar1=a1, scalar2=a2, op0=op0, **kw))
+
+    def tt(out, a, b, o, off=None):
+        src = ap(a) if off is None else ap(a).indirect(ap(off))
+        op("v", [out], [a, b] + ([off] if off else []), lambda e: e.tensor_tensor(out=ap(out), in0=src, in1=ap(b), op=o))
+
+    def cp(out, i, off=None, scatter=None):
+        src = ap(i) if off is None else ap(i).indirect(ap(off))
+        dst = ap(out) if scatter is None else ap(out).indirect(ap(scatter))
+        op("v", [out], [i] + [o for o in (off, scatter) if o], lambda e: e.tensor_copy(out=dst, in_=src))
+
+    def scan(out, a, b, o0, o1):
+        op("v", [out], [a, b], lambda e: e.tensor_tensor_scan(out=ap(out), data0=ap(a), data1=ap(b), initial=0.0, op0=o0, op1=o1))
+
+    def red(out, i, o):
+        op("v", [out], [i], lambda e: e.tensor_reduce(out=ap(out), in_=ap(i), axis=AxisListType.X, op=o))
+
+    def fill(out, c):
+        op("v", [out], [], lambda e: e.memset(ap(out), c))
+
+    def act(out, i, fn, bias=None, scale=None, accum=None, off=None):
+        src = ap(i) if off is None else ap(i).indirect(ap(off))
+        kw = {}
+        if bias is not None:
+            kw["bias"] = ap(bias) if isinstance(bias, tuple) else bias
+        if scale is not None:
+            kw["scale"] = scale
+        if accum is not None:
+            kw["accum_out"] = ap(accum)
+        op("s", [out] + ([accum] if accum else []), [i] + [o for o in (bias, off) if isinstance(o, tuple)],
+           lambda e: e.activation(out=ap(out), in_=src, func=fn, **kw))
+
+    def quant(q, s, i):
+        op("v", [q, s], [i], lambda e: e.quantize_mx(ap(q), ap(s), ap(i)))
+
+    def mm(out, l, ls, r, rs, start=True, stop=True):
+        op("t", [out], [l, ls, r, rs], lambda e: e.matmul_mx(ap(out), ap(l), ap(ls), ap(r), ap(rs), start, stop), not start)
+
+    def iota(out, pattern, base, cm, flag=False):
+        kw = {"allow_small_or_imprecise_dtypes": True} if flag else {}
+        op("g", [out], [], lambda e: e.iota(ap(out), pattern, base, cm, **kw))
+
+    def select(out, i, pattern, cmp, c, base, cm):
+        op("g", [out], [i], lambda e: e.affine_select(ap(out), ap(i), pattern, cmp, c, base, cm))
+
+    def col(n):
+        return R(n, 0, 1)
+
+    def planes(x):
+        for b in range(4):
+            act(R("xp", 256 * b, 256 * b + 256), R(x, b, 1024, 4), F.Copy)
+
+    dma("y", ap(R("xi0")), T.x[:], [R("xi0")])
+    dma("s", ap(R("ub")), T.u[:], [R("ub")])
+    dma("y", ap(R("wq")).bitcast(dt.uint8), T.wc[:], [R("wq")])
+    dma("y", ap(R("wsc")), T.ws[:], [R("wsc")])
+    dma("y", ap(R("vb")), T.v[:], [R("vb")])
+    iota(R("iP"), [[0, 2]], 0, 1)
+    iota(R("iL"), [[16, 8]], 0, 0)
+    iota(R("fI"), [[1, 256]], 0, 0, True)
+    iota(R("iD"), [[0, 16], [1, 16]], 128, -1)
+    act(R("bigt"), R("fI"), F.Identity, bias=BIG, scale=0.0)
+    act(R("cme", 1, 1024, 4), R("fI"), F.Copy, scale=0.0)
+    act(R("cme", 2, 1024, 4), R("fI"), F.Copy, scale=0.0)
+    act(R("cme", 3, 1024, 4), R("fI"), F.Copy, scale=0.0)
+    iota(R("iC"), [[1, 8], [0, 64]], 0, 0)
+    select(R("d0"), R("bigt"), [[0, 16], [1, 16]], A.is_equal, -BIG, 0, 0)
+    iota(R("c16"), [[16, 16]], -1, 0, True)
+    iota(R("ek"), [[1, 2056]], 0, 0, True)
+    iota(R("iS"), [[0, 4], [16, 4]], 0, 1)
+    iota(R("k16"), [[16, 4], [0, 4]], 0, 0, True)
+    for c, k in enumerate((1, 3, 2, 0)):
+        iota(R("tb", 64 * c, 64 * c + 64), [[1, 64]], 64 * k, 0, True)
+    for a in range(4):
+        fill(R("cm%d" % a, 4 * 16 * (4 * a + 1), 4 * WD[a]), 0.0)
+    fill(R("rs", 0, 1), 0.0)
+    ts(R("pq"), R("iP"), 15, A.bitwise_and)
+    ts(R("pc"), R("pq"), 2, A.arith_shift_right)
+    cp(R("cf"), R("pc"))
+    ts(R("ch"), R("cf"), 2.0, A.is_ge)
+    ts(R("ca1"), R("cf"), 2.0, A.mult, 1.0, A.add)
+    ts(R("ca2"), R("cf"), 4.0, A.mult, -5.0, A.add)
+    tt(R("ca3"), R("ca2"), R("ch"), A.mult)
+    tt(R("kf"), R("ca1"), R("ca3"), A.subtract)
+    ts(R("ul", 0, 8), R("iL"), 4.0, A.add)
+    ts(R("ul", 8, 16), R("iL"), col("kf"), A.add)
+    ts(R("dl"), R("iD"), 15, A.bitwise_and)
+    ts(R("kk01"), R("dl"), 0.0, A.is_gt, 2.0 * BIG, A.mult)
+    act(R("maskb"), R("kk01"), F.Identity, bias=-BIG)
+    ts(R("pg"), R("iP"), 4, A.arith_shift_right)
+    cp(R("gpf"), R("pg"))
+    quant(R("qu"), R("su"), R("ub"))
+    op("v", [R("qu2")], [R("qu"), R("ul")],
+       lambda e: e.tensor_copy(ap(R("qu2")).bitcast(dt.uint32), ap(R("qu")).bitcast(dt.uint32).indirect(ap(R("ul")))))
+    act(R("su2"), R("su"), F.Copy, off=R("ul"))
+    act(R("io20"), R("fI"), F.Copy, scale=2.0 ** -20)
+    act(R("ones"), R("fI"), F.Identity, bias=1.0, scale=0.0)
+    quant(R("qx0"), R("sx0"), R("xi0"))
+    planes("xi0")
+    ts(R("gt"), R("iC"), col("gpf"), A.is_equal)
+    quant(R("qg"), R("sg"), R("gt"))
+
+    def late_constants():
+        ts(R("kc0"), R("kf"), -1.0, A.mult, 1027.0, A.add)
+        ts(R("pgf"), R("gpf"), 16.0, A.mult)
+        ts(R("s16p"), R("iS"), col("pgf"), A.subtract, 1.0, A.add)
+        for b in range(4):
+            fill(R("xs", PT * b, PT * b + 1), 0.0)
+            fill(R("xs", PT * b + 257, PT * b + PT), 0.0)
+        fill(R("hf"), 0.5)
+        select(R("ex"), R("hf"), [[-1, 516]], A.is_equal, 0.0, 3, 4)
+
+    def later_constants():
+        for b in range(4):
+            fill(R("dwn", PD * b + 256, PD * b + PD), 0.0)
+        fill(R("tb", 256, 264), -1.0)
+        quant(R("qv"), R("sv"), R("vb"))
+
+    rel = _relays(topo, T.cores, rank)
+    nloc = [0]
+
+    def view(n, a, b, w):
+        v = T[n][:, a:b]
+        return v.bitcast(dt.uint8) if w == "c" else v
+
+    def send_two(ph, w, src, t):
+        before("g", (), [R(src)], "remote")
+        tr = []
+        for i in range(2):
+            rid, pid = topo.addr(rel[i], core)
+            en = topo.engines(core, rel[i])
+            h = len(en) // 2
+            en = en[i * h:i * h + h]
+            tr.append(RemoteDMATransfer(dst_ids=[DstId(rid=rid, pnc=pid)], dma_engine_mask=_mask(en), remote_sem=T.sem["r%s%s%d" % (w, ph, t)],
+                                        src=view(src, 64 * i, 64 * i + 64, w), dst=view("r%s%s%d" % (ph, w, t), 0, 64, w)))
+            nloc[0] += h
+        g.remote_dma_fused(tr, local_sem=T.sem.loc)
+
+    def send_one(ph, w, src, a, dst, to, land, t):
+        before("g", (), [R(src, a, a + 64)], "remote")
+        rid, pid = topo.addr(dst, core)
+        en = topo.engines(core, dst)
+        g.remote_dma(out_ap=view(land, to, to + 64, w), in_ap=view(src, a, a + 64, w), remote_sem=T.sem["ad%s%d" % (ph, t)],
+                     local_sem=T.sem.loc, pid=pid, routing_id=rid, dma_engine_mask=_mask(en))
+        nloc[0] += len(en)
+
+    def layer(qb, sb, off, z, qz, sz, h, qh, sh, hoff):
+        for b in range(4):
+            mm(R("pd", 512 * b, 512 * b + 128), R("qe%d" % b), R("se%d" % b), R(qb, off, off + 128), R(sb, off, off + 128))
+        for b in range(4):
+            tt(R(z, b, 512, 4), R("pd", 512 * b, 512 * b + 128), R("e2x", 128 * b, 128 * b + 128), A.add)
+        quant(R(qz), R(sz), R(z))
+        for b in (2, 0, 3, 1):
+            mm(R("pr", 512 * b, 512 * b + 128), R("wq", 128 * b, 128 * b + 128), R("wsc", 128 * b, 128 * b + 128), R(qz), R(sz))
+        for b in (2, 0, 3, 1):
+            o, i = R(h, b, 512, 4), R("pr", 512 * b, 512 * b + 128)
+            if b < 2:
+                ts(o, i, 0.03125, A.mult)
+            else:
+                act(o, i, F.Copy, scale=0.03125)
+        quant(R(qh, hoff, hoff + 128), R(sh, hoff, hoff + 128), R(h))
+
+    def unpack(q, s, off, to):
+        for b in (2, 0, 3, 1):
+            mm(R("pd", 512 * b, 512 * b + 128), R("qe%d" % b), R("se%d" % b), R(q, off, off + 128), R(s, off, off + 128))
+        for b in (2, 0, 3, 1):
+            o, i = R("dwn", PD * b + to, PD * b + to + 128), R("pd", 512 * b, 512 * b + 128)
+            if b < 2:
+                ts(o, i, 2.0, A.mult)
+            else:
+                act(o, i, F.Copy, scale=2.0)
+
+    def count(n, m, bias):
+        act(R("junk2", 256 * n - 256, 256 * n), R("cum"), F.Sign, bias=bias, scale=-float(m), accum=col("ac%d" % n))
+
+    def answer(n, kc):
+        ts(col("ky%d" % n), col("ac%d" % n), -4.0, A.mult, col(kc), A.add)
+        cp(R("ck%d" % n), R("ek"), off=col("ky%d" % n))
+        red(col("km%d" % n), R("ck%d" % n), A.max)
+
+    def place(n):
+        ts(col("ao%d" % n), col("km%d" % n), -0.125, A.mult, 256.375, A.add)
+
+    for t in range(2):
+        X, Q, S = "xi%d" % t, "qx%d" % t, "sx%d" % t
+        pa, pv, pc = R("pr", 0, 256), R("pr", 512, 768), R("pr", 1024, 1280)
+        mm(pa, R("qu2", 0, 128), R("su2", 0, 128), R(Q), R(S))
+        mm(pv, R("qu2", 128, 256), R("su2", 128, 256), R(Q), R(S))
+        act(R("sg1"), pv, F.Sign)
+        act(R("sg2"), R("sg1"), F.Relu)
+        tt(R("dd"), pa, R("maskb"), A.max)
+        scan(R("ow"), R("d0"), R("dd"), A.max, A.min)
+        tt(R("cme", 0, 1024, 4), pa, R("ow"), A.is_equal)
+        quant(R("qce"), R("sce"), R("cme"))
+        mm(pc, R("qg"), R("sg"), R("qce"), R("sce"), True, False)
+        for a in (3, 2, 1, 0):
+            for e in (3, 2, 1, 0):
+                m = 4 * a + e
+                ts(R("cm%d" % a, e, 64 * m + 64, 4), R("pr", 0, 16 * m + 16), R("ow", 16 * m + 15, 16 * m + 16), A.is_lt)
+                if m:
+                    act(R("junk", 8 * m * (m - 1), 8 * m * (m + 1)), R("cm%d" % a, e, 64 * m, 4), F.Copy, accum=R("rs", m, m + 1))
+            quant(R("qc%d" % a), R("sc%d" % a), R("cm%d" % a))
+            mm(R("pr", 1024, 1024 + WD[a]), R("qg"), R("sg"), R("qc%d" % a), R("sc%d" % a), False, a == 0)
+        tt(R("pay"), R("sg2"), R("io20"), A.add)
+        tt(R("rt"), R("rs"), R("c16"), A.subtract)
+        tt(R("dw2"), pc, R("maskb"), A.max)
+        scan(R("ow2"), R("d0"), R("dw2"), A.max, A.min)
+        tt(R("rk"), R("ow2", 15, 256, 16), R("rt"), A.subtract)
+        cp(R("ro"), R("rk"))
+        cp(R("win"), R("pay"), scatter=R("ro"))
+        scan(R("cum"), R("win"), R("ones"), A.add, A.add)
+        ts(col("tm"), R("cum", 255, 256), -0.5, A.add)
+        count(1, 4, col("tm"))
+        if t == 0:
+            late_constants()
+        tt(R("dw3"), R("win"), R("maskb"), A.max)
+        answer(1, "kc0")
+        place(1)
+        ts(R("bs2"), R("cum"), 2.0, A.mult, col("tm"), A.add, off=col("ao1"))
+        count(2, 3, R("bs2", 0, 1))
+        scan(R("ow3"), R("d0"), R("dw3"), A.max, A.min)
+        ts(col("kx1"), col("ky1"), col("km1"), A.is_equal, -5000.0, A.mult)
+        tt(col("kcb"), col("kx1"), col("kc0"), A.add)
+        answer(2, "kcb")
+        place(2)
+        ts(R("bs3"), R("cum"), 1.0, A.mult, col("tm"), A.add, off=col("ao2"))
+        count(3, 2, R("bs3", 0, 1))
+        ts(R("bt"), R("ow3", 15, 256, 16), 1.0, A.is_ge)
+        tt(R("io"), R("ow3", 15, 256, 16), R("bt"), A.subtract)
+        ts(R("ol"), R("io"), 2.0 ** 20, A.mult)
+        for b in range(4):
+            act(R("xs", PT * b + 1, PT * b + 257), R("xp", 256 * b, 256 * b + 256), F.Copy, off=R("ol"))
+        ts(col("kx2"), col("ky2"), col("km2"), A.is_equal, -5000.0, A.mult)
+        tt(col("kcc"), col("kx2"), col("kcb"), A.add)
+        ts(R("w1"), R("ck1"), col("km1"), A.is_equal)
+        ts(R("w2"), R("ck2"), col("km2"), A.is_equal)
+        ts(col("fr1"), col("km1"), -0.125, A.mult, 257.375, A.add)
+        ts(col("fr2"), col("km2"), -0.125, A.mult, 257.375, A.add)
+        ts(R("t1"), R("w2"), col("fr1"), A.mult)
+        tt(R("t1"), R("t1"), R("s16p"), A.add)
+        ts(col("e1"), col("fr1"), -999.5, A.add)
+        ts(col("e2"), col("fr2"), -999.5, A.add)
+        ts(R("xa"), R("w1"), col("e1"), A.mult, 1000.0, A.add)
+        ts(R("xb"), R("w2"), col("e2"), A.mult)
+        tt(R("xa"), R("xa"), R("xb"), A.add)
+        tt(R("xc"), R("w1"), R("w2"), A.add)
+        ts(R("xc"), R("xc"), -1.0, A.mult, 1.0, A.add)
+        answer(3, "kcc")
+        ts(col("fr3"), col("km3"), -0.125, A.mult, 257.375, A.add)
+        ts(col("dda"), col("fr3"), -1.0, A.mult, col("fr2"), A.add)
+        ts(col("em"), col("fr3"), -999.5, A.add)
+        ts(R("t2"), R("ck3"), col("km3"), A.is_equal, col("dda"), A.mult)
+        ts(R("t3"), R("xc"), col("fr3"), A.mult)
+        tt(R("t1"), R("t1"), R("t2"), A.add)
+        ts(R("en"), R("ck3"), col("km3"), A.is_equal, col("em"), A.mult)
+        tt(R("t1"), R("t1"), R("t3"), A.add)
+        tt(R("en"), R("en"), R("xa"), A.add)
+        tt(R("vl"), R("t1"), R("en"), A.is_lt)
+        tt(R("plf"), R("t1"), R("vl"), A.mult)
+        cp(R("pl"), R("plf"))
+        for o, lo, q, s in (("b13", 0, "qb%d" % t, "sb%d" % t), ("b02", 8, "wbc%d" % t, "wbs%d" % t)):
+            for b in (2, 0, 3, 1):
+                if b < 2:
+                    cp(R(o, b, 512, 4), R("xs", PT * b, PT * b + PT), off=R("pl", lo, lo + 8))
+                else:
+                    act(R(o, b, 512, 4), R("xs", PT * b, PT * b + PT), F.Copy, off=R("pl", lo, lo + 8))
+            quant(R(q, 0, 128), R(s, 0, 128), R(o))
+            if lo == 0:
+                send_two("b", "c", q, t)
+                send_two("b", "s", s, t)
+        d2 = T.cores[(rank + 2) % N]
+        send_one("b", "c", "wbc%d" % t, 0, d2, 128, "wbc%d" % t, t)
+        send_one("b", "s", "wbs%d" % t, 0, d2, 128, "wbs%d" % t, t)
+        for b in range(4):
+            for k in range(2):
+                act(R("e2x", 128 * b + 64 * k, 128 * b + 64 * k + 64), R("xs", PT * b + 1, PT * b + 65), F.Copy, scale=0.5)
+        if t == 0:
+            for b in range(4):
+                quant(R("qe%d" % b), R("se%d" % b), R("ex", 3 - b, 515 - b))
+        lands("adb%d" % t, 16, [R("wbc%d" % t, 128, 192), R("wbs%d" % t, 128, 192)])
+        lands("aob%d" % t, 32, [R("lbc%d" % t), R("lbs%d" % t)])
+        layer("wbc%d" % t, "wbs%d" % t, 64, "za", "qza", "sza", "ha", "whc%d" % t, "whs%d" % t, 64)
+        p2 = T.cores[(rank - 2) % N]
+        send_one("h", "c", "whc%d" % t, 128, p2, 0, "whc%d" % t, t)
+        send_one("h", "s", "whs%d" % t, 128, p2, 0, "whs%d" % t, t)
+        layer("lbc%d" % t, "lbs%d" % t, 0, "zb", "qzb", "szb", "hb", "qh%d" % t, "sh%d" % t, 0)
+        send_two("h", "c", "qh%d" % t, t)
+        send_two("h", "s", "sh%d" % t, t)
+        if t == 0:
+            later_constants()
+        place(3)
+        ts(R("w3"), R("ck3"), col("km3"), A.is_equal)
+        for n in (1, 2, 3):
+            ts(col("af%d" % n), col("ao%d" % n), 1.0, A.add)
+            tt(R("c%d" % n), R("w%d" % n), R("k16"), A.mult)
+            red(col("cb%d" % n), R("c%d" % n), A.add)
+        tt(col("cb4"), col("cb1"), col("cb2"), A.add)
+        tt(col("cb4"), col("cb4"), col("cb3"), A.add)
+        ts(col("cb4"), col("cb4"), -1.0, A.mult, 384.0, A.add)
+        for n in (2, 3, 4):
+            tt(col("db%d" % n), col("cb%d" % n), col("cb%d" % (n - 1)), A.subtract)
+        tt(col("da2"), col("af2"), col("af1"), A.subtract)
+        tt(col("da3"), col("af3"), col("af2"), A.subtract)
+        for n, d in ((1, "af1"), (2, "da2"), (3, "da3")):
+            ts(R("y%d" % n), R("rk"), col("af%d" % n), A.is_ge, col(d), A.mult)
+            ts(R("z%d" % n), R("rk"), col("af%d" % n), A.is_ge, col("db%d" % (n + 1)), A.mult)
+        tt(R("rl"), R("rk"), R("y1"), A.subtract)
+        tt(R("rl"), R("rl"), R("y2"), A.subtract)
+        tt(R("rl"), R("rl"), R("y3"), A.subtract)
+        ts(R("sv1"), R("rl"), col("cb1"), A.add, -256.0, A.add)
+        for n in (1, 2, 3):
+            tt(R("sv1"), R("sv1"), R("z%d" % n), A.add)
+        ts(R("vl"), R("rl"), 64.0, A.is_lt)
+        tt(R("sf"), R("sv1"), R("vl"), A.mult)
+        ts(R("so"), R("sf"), 256.0, A.add)
+        if t == 1:
+            act(R("slr"), R("tb"), F.Copy, off=R("so"))
+            dma("y", T.sl[:], T.slr[0:128:16, :], (), [R("slr")])
+        lands("adh%d" % t, 16, [R("whc%d" % t, 0, 64), R("whs%d" % t, 0, 64)])
+        lands("aoh%d" % t, 32, [R("lhc%d" % t), R("lhs%d" % t)])
+        unpack("whc%d" % t, "whs%d" % t, 0, 128)
+        unpack("lhc%d" % t, "lhs%d" % t, 0, 0)
+        X2 = "xi%d" % (t + 1)
+        for b in range(4):
+            tt(R(X2, b, 1024, 4), R("dwn", PD * b, PD * b + PD), R(X, b, 1024, 4), A.add, off=R("so"))
+        quant(R("qx%d" % (t + 1)), R("sx%d" % (t + 1)), R(X2))
+        if t == 0:
+            planes(X2)
+    mm(R("pr", 0, 256), R("qv"), R("sv"), R("qx2"), R("sx2"))
+    dma("y", T.oc[:], ap(R("qx2")).bitcast(dt.uint8), (), [R("qx2")])
+    for k in range(4):
+        dma("s" if k % 2 else "y", T.osc[4 * k:4 * k + 4, :], T.sx2[32 * k:32 * k + 4, :], (), [R("sx2")])
+    act(R("ycp"), R("pr", 0, 256), F.Copy)
+    dma("s", T.y[:], ap(R("ycp")), (), [R("ycp")])
+    tot["loc"] = nloc[0]
+    for sem in sorted(tot):
+        wait("g", sem, tot[sem])

@@ -3,7 +3,8 @@ from concourse.mybir import dt, AluOpType as A, AxisListType, ActivationFunction
 
 N = 8
 BIG = float(2.0 ** 90)
-PT = 320
+PT = 336
+NO = 320
 PD = 272
 WD = (128, 128, 192, 256)
 SCRATCH = {}
@@ -41,7 +42,8 @@ def _decl():
     add("cme", 1024, b)
     share("qc", q, ("qc0 qc1", 128), ("qc2", 192), ("qc3 qce", 256)), share("sc", s, ("sc0 sc1", 128), ("sc2", 192), ("sc3 sce", 256))
     add("dd ow sg1 sg2 pay dw2 ow2 win cum dw3 ow3 ycp slr", 256, f), add("junk", 1920, b), add("junk2", 768, b)
-    share("sm", f, ("rs rt rk ck1 ck2 ck3 bs2 bs3 bt io w1 w2 w3 xa xb xc t1 t2 t3 en vl plf c1 c2 c3 z1 z2 z3 y1 y2 y3 sv1 rl sf", 16),
+    add("rl13 rl14 rl15", 256, b)
+    share("sm", f, ("rs rt rk ck1 ck2 ck3 bs2 bs3 bt io w1 w2 w3 xa xb t1 t2 t3 en vl plf c1 c2 c3 z1 z2 z3 y1 y2 y3 sv1 rl sf", 16),
           ("tm ac1 ac2 ac3 km1 km2 km3 kx1 kx2 kcb kcc fr1 fr2 fr3 dda em af1 af2 af3 cb1 cb2 cb3 cb4 db2 db3 db4 da2 da3 e1 e2", 2))
     share("li", h, ("ro pl so ol", 16), ("ky1 ky2 ky3 ao1 ao2 ao3", 2))
     add("xp", 1024, b), add("xs", 4 * PT, b), add("e2x", 512, b), add("dwn", 4 * PD, b)
@@ -63,14 +65,15 @@ SEMAPHORES = ["ev", "es", "et", "eg", "loc"] + ["d%d" % k for k in range(14)] + 
 def _relays(topo, cores, r):
     c = cores[r]
     own = [d for d in topo.cores_of(c) if d != c and topo.may_write(d, cores[(r + 1) % N]) and topo.may_write(d, cores[(r + 3) % N])]
-    return [[d for d in own if topo.die(d) == topo.die(c)][0], [d for d in own if topo.die(d) != topo.die(c)][0]]
+    near, far = [[d for d in own if (topo.die(d) == topo.die(c)) == same] for same in (True, False)]
+    return [(near[0], "c", 0), (near[-1], "s", 0), (far[0], "c", 1), (far[-1], "s", 1)]
 
 
 def _mask(engines):
     return sum(1 << int(e) for e in engines)
 
 
-def _relay(g, core, T, topo, r, i):
+def _relay(g, core, T, topo, r, w, i):
     n = 0
     for t in range(2):
         for ph in "bh":
@@ -78,14 +81,13 @@ def _relay(g, core, T, topo, r, i):
             dst = T.cores[(r + (k if ph == "b" else -k)) % N]
             rid, pid = topo.addr(dst, core)
             en = topo.engines(core, dst)
-            for w in "cs":
-                g.wait_ge(T.sem["r%s%s%d" % (w, ph, t)], 8)
-                src, d = T["r%s%s%d" % (ph, w, t)][:, 0:64], T["l%s%s%d" % (ph, w, t)][:, 64 * i:64 * i + 64]
-                if w == "c":
-                    src, d = src.bitcast(dt.uint8), d.bitcast(dt.uint8)
-                g.remote_dma(out_ap=d, in_ap=src, remote_sem=T.sem["ao%s%d" % (ph, t)], local_sem=T.sem.loc, pid=pid, routing_id=rid,
-                             dma_engine_mask=_mask(en))
-                n += len(en)
+            g.wait_ge(T.sem["r%s%s%d" % (w, ph, t)], 8)
+            src, d = T["r%s%s%d" % (ph, w, t)][:, 0:64], T["l%s%s%d" % (ph, w, t)][:, 64 * i:64 * i + 64]
+            if w == "c":
+                src, d = src.bitcast(dt.uint8), d.bitcast(dt.uint8)
+            g.remote_dma(out_ap=d, in_ap=src, remote_sem=T.sem["ao%s%d" % (ph, t)], local_sem=T.sem.loc, pid=pid, routing_id=rid,
+                         dma_engine_mask=_mask(en))
+            n += len(en)
     g.wait_ge(T.sem.loc, n)
 
 
@@ -94,9 +96,9 @@ def rank_program(g, core, T, topo):
     if rank is None:
         for r in range(N):
             if core in topo.cores_of(T.cores[r]):
-                rel = _relays(topo, T.cores, r)
-                if core in rel:
-                    _relay(g, core, T, topo, r, rel.index(core))
+                for d, w, i in _relays(topo, T.cores, r):
+                    if d == core:
+                        _relay(g, core, T, topo, r, w, i)
         return
     eng = {"v": g.vector, "s": g.scalar, "t": g.tensor, "g": g, "y": g.sync}
     seen = {q: {} for q in eng}
@@ -236,9 +238,8 @@ def rank_program(g, core, T, topo):
     iota(R("fI"), [[1, 256]], 0, 0, True)
     iota(R("iD"), [[0, 16], [1, 16]], 128, -1)
     act(R("bigt"), R("fI"), F.Identity, bias=BIG, scale=0.0)
-    act(R("cme", 1, 1024, 4), R("fI"), F.Copy, scale=0.0)
-    act(R("cme", 2, 1024, 4), R("fI"), F.Copy, scale=0.0)
-    act(R("cme", 3, 1024, 4), R("fI"), F.Copy, scale=0.0)
+    for b in (1, 2, 3):
+        act(R("cme", b, 1024, 4), R("fI"), F.Copy, scale=0.0)
     iota(R("iC"), [[1, 8], [0, 64]], 0, 0)
     select(R("d0"), R("bigt"), [[0, 16], [1, 16]], A.is_equal, -BIG, 0, 0)
     iota(R("c16"), [[16, 16]], -1, 0, True)
@@ -272,17 +273,15 @@ def rank_program(g, core, T, topo):
     act(R("io20"), R("fI"), F.Copy, scale=2.0 ** -20)
     act(R("ones"), R("fI"), F.Identity, bias=1.0, scale=0.0)
     quant(R("qx0"), R("sx0"), R("xi0"))
-    planes("xi0")
     ts(R("gt"), R("iC"), col("gpf"), A.is_equal)
     quant(R("qg"), R("sg"), R("gt"))
 
     def late_constants():
         ts(R("kc0"), R("kf"), -1.0, A.mult, 1027.0, A.add)
         ts(R("pgf"), R("gpf"), 16.0, A.mult)
-        ts(R("s16p"), R("iS"), col("pgf"), A.subtract, 1.0, A.add)
+        ts(R("s16p"), R("iS"), col("pgf"), A.subtract, -float(NO), A.add)
         for b in range(4):
-            fill(R("xs", PT * b, PT * b + 1), 0.0)
-            fill(R("xs", PT * b + 257, PT * b + PT), 0.0)
+            fill(R("xs", PT * b + 256, PT * b + PT), 0.0)
         fill(R("hf"), 0.5)
         select(R("ex"), R("hf"), [[-1, 516]], A.is_equal, 0.0, 3, 4)
 
@@ -292,7 +291,7 @@ def rank_program(g, core, T, topo):
         fill(R("tb", 256, 264), -1.0)
         quant(R("qv"), R("sv"), R("vb"))
 
-    rel = _relays(topo, T.cores, rank)
+    rel = {(w, i): d for d, w, i in _relays(topo, T.cores, rank)}
     nloc = [0]
 
     def view(n, a, b, w):
@@ -303,8 +302,8 @@ def rank_program(g, core, T, topo):
         before("g", (), [R(src)], "remote")
         tr = []
         for i in range(2):
-            rid, pid = topo.addr(rel[i], core)
-            en = topo.engines(core, rel[i])
+            rid, pid = topo.addr(rel[(w, i)], core)
+            en = topo.engines(core, rel[(w, i)])
             h = len(en) // 2
             en = en[i * h:i * h + h]
             tr.append(RemoteDMATransfer(dst_ids=[DstId(rid=rid, pnc=pid)], dma_engine_mask=_mask(en), remote_sem=T.sem["r%s%s%d" % (w, ph, t)],
@@ -354,6 +353,10 @@ def rank_program(g, core, T, topo):
         cp(R("ck%d" % n), R("ek"), off=col("ky%d" % n))
         red(col("km%d" % n), R("ck%d" % n), A.max)
 
+    def edge(n):
+        act(col("fr%d" % n), col("km%d" % n), F.Identity, bias=257.375, scale=-0.125)
+        act(col("e%d" % n), col("km%d" % n), F.Identity, bias=256.875 - NO, scale=-0.125)
+
     def place(n):
         ts(col("ao%d" % n), col("km%d" % n), -0.125, A.mult, 256.375, A.add)
 
@@ -362,21 +365,33 @@ def rank_program(g, core, T, topo):
         pa, pv, pc = R("pr", 0, 256), R("pr", 512, 768), R("pr", 1024, 1280)
         mm(pa, R("qu2", 0, 128), R("su2", 0, 128), R(Q), R(S))
         mm(pv, R("qu2", 128, 256), R("su2", 128, 256), R(Q), R(S))
+        mm(R("pr", 1536, 1792), R("qu2", 0, 128), R("su2", 0, 128), R(Q), R(S))
         act(R("sg1"), pv, F.Sign)
         act(R("sg2"), R("sg1"), F.Relu)
         tt(R("dd"), pa, R("maskb"), A.max)
         scan(R("ow"), R("d0"), R("dd"), A.max, A.min)
+        share = (15, 14) if t == 0 else (15, 14, 13)
+        for m in share:
+            own, e, n = R("ow", 16 * m + 15, 16 * m + 16), m - 12, 16 * m
+            act(R("rl%d" % m, 0, n + 16), R("pr", 1536, 1552 + n), F.Relu, bias=own, scale=-1.0)
+            act(R("cm3", e, 4 * n, 4), R("rl%d" % m, 0, n), F.Sign, accum=R("rs", m, m + 1))
+            act(R("cm3", 4 * n + e, 4 * n + 64, 4), R("rl%d" % m, n, n + 16), F.Sign)
         tt(R("cme", 0, 1024, 4), pa, R("ow"), A.is_equal)
         quant(R("qce"), R("sce"), R("cme"))
         mm(pc, R("qg"), R("sg"), R("qce"), R("sce"), True, False)
-        for a in (3, 2, 1, 0):
-            for e in (3, 2, 1, 0):
-                m = 4 * a + e
+        for m in (13, 12, 11, 10, 9, 8, "q2", 7, 6, 5, 4, "q1", "q3", 3, 2, 1, 0, "q0"):
+            if m in share:
+                continue
+            if isinstance(m, int):
+                a, e = m // 4, m % 4
                 ts(R("cm%d" % a, e, 64 * m + 64, 4), R("pr", 0, 16 * m + 16), R("ow", 16 * m + 15, 16 * m + 16), A.is_lt)
                 if m:
                     act(R("junk", 8 * m * (m - 1), 8 * m * (m + 1)), R("cm%d" % a, e, 64 * m, 4), F.Copy, accum=R("rs", m, m + 1))
-            quant(R("qc%d" % a), R("sc%d" % a), R("cm%d" % a))
-            mm(R("pr", 1024, 1024 + WD[a]), R("qg"), R("sg"), R("qc%d" % a), R("sc%d" % a), False, a == 0)
+            else:
+                a = int(m[1])
+                quant(R("qc%d" % a), R("sc%d" % a), R("cm%d" % a))
+                mm(R("pr", 1024, 1024 + WD[a]), R("qg"), R("sg"), R("qc%d" % a), R("sc%d" % a), False, a == 0)
+        planes(X)
         tt(R("pay"), R("sg2"), R("io20"), A.add)
         tt(R("rt"), R("rs"), R("c16"), A.subtract)
         tt(R("dw2"), pc, R("maskb"), A.max)
@@ -391,49 +406,43 @@ def rank_program(g, core, T, topo):
             late_constants()
         tt(R("dw3"), R("win"), R("maskb"), A.max)
         answer(1, "kc0")
+        edge(1)
         place(1)
         ts(R("bs2"), R("cum"), 2.0, A.mult, col("tm"), A.add, off=col("ao1"))
         count(2, 3, R("bs2", 0, 1))
-        scan(R("ow3"), R("d0"), R("dw3"), A.max, A.min)
         ts(col("kx1"), col("ky1"), col("km1"), A.is_equal, -5000.0, A.mult)
         tt(col("kcb"), col("kx1"), col("kc0"), A.add)
+        scan(R("ow3"), R("d0"), R("dw3"), A.max, A.min)
         answer(2, "kcb")
+        edge(2)
         place(2)
         ts(R("bs3"), R("cum"), 1.0, A.mult, col("tm"), A.add, off=col("ao2"))
         count(3, 2, R("bs3", 0, 1))
         ts(R("bt"), R("ow3", 15, 256, 16), 1.0, A.is_ge)
+        ts(col("kx2"), col("ky2"), col("km2"), A.is_equal, -5000.0, A.mult)
         tt(R("io"), R("ow3", 15, 256, 16), R("bt"), A.subtract)
+        tt(col("kcc"), col("kx2"), col("kcb"), A.add)
         ts(R("ol"), R("io"), 2.0 ** 20, A.mult)
         for b in range(4):
-            act(R("xs", PT * b + 1, PT * b + 257), R("xp", 256 * b, 256 * b + 256), F.Copy, off=R("ol"))
-        ts(col("kx2"), col("ky2"), col("km2"), A.is_equal, -5000.0, A.mult)
-        tt(col("kcc"), col("kx2"), col("kcb"), A.add)
-        ts(R("w1"), R("ck1"), col("km1"), A.is_equal)
-        ts(R("w2"), R("ck2"), col("km2"), A.is_equal)
-        ts(col("fr1"), col("km1"), -0.125, A.mult, 257.375, A.add)
-        ts(col("fr2"), col("km2"), -0.125, A.mult, 257.375, A.add)
-        ts(R("t1"), R("w2"), col("fr1"), A.mult)
+            act(R("xs", PT * b, PT * b + 256), R("xp", 256 * b, 256 * b + 256), F.Copy, off=R("ol"))
+        ts(R("t1"), R("ck2"), col("km2"), A.is_equal, col("fr1"), A.mult)
+        ts(R("xa"), R("ck1"), col("km1"), A.is_equal, col("e1"), A.mult)
+        ts(R("xb"), R("ck2"), col("km2"), A.is_equal, col("e2"), A.mult)
         tt(R("t1"), R("t1"), R("s16p"), A.add)
-        ts(col("e1"), col("fr1"), -999.5, A.add)
-        ts(col("e2"), col("fr2"), -999.5, A.add)
-        ts(R("xa"), R("w1"), col("e1"), A.mult, 1000.0, A.add)
-        ts(R("xb"), R("w2"), col("e2"), A.mult)
         tt(R("xa"), R("xa"), R("xb"), A.add)
-        tt(R("xc"), R("w1"), R("w2"), A.add)
-        ts(R("xc"), R("xc"), -1.0, A.mult, 1.0, A.add)
         answer(3, "kcc")
         ts(col("fr3"), col("km3"), -0.125, A.mult, 257.375, A.add)
+        ts(col("em"), col("km3"), -0.125, A.mult, 256.875 - NO, A.add)
         ts(col("dda"), col("fr3"), -1.0, A.mult, col("fr2"), A.add)
-        ts(col("em"), col("fr3"), -999.5, A.add)
-        ts(R("t2"), R("ck3"), col("km3"), A.is_equal, col("dda"), A.mult)
-        ts(R("t3"), R("xc"), col("fr3"), A.mult)
-        tt(R("t1"), R("t1"), R("t2"), A.add)
+        ts(R("t3"), R("ck3"), 0.0, A.is_gt, col("fr3"), A.mult)
         ts(R("en"), R("ck3"), col("km3"), A.is_equal, col("em"), A.mult)
+        ts(R("t2"), R("ck3"), col("km3"), A.is_equal, col("dda"), A.mult)
         tt(R("t1"), R("t1"), R("t3"), A.add)
         tt(R("en"), R("en"), R("xa"), A.add)
+        tt(R("t1"), R("t1"), R("t2"), A.add)
         tt(R("vl"), R("t1"), R("en"), A.is_lt)
         tt(R("plf"), R("t1"), R("vl"), A.mult)
-        cp(R("pl"), R("plf"))
+        ts(R("pl"), R("plf"), float(NO), A.add)
         for o, lo, q, s in (("b13", 0, "qb%d" % t, "sb%d" % t), ("b02", 8, "wbc%d" % t, "wbs%d" % t)):
             for b in (2, 0, 3, 1):
                 if b < 2:
@@ -449,7 +458,7 @@ def rank_program(g, core, T, topo):
         send_one("b", "s", "wbs%d" % t, 0, d2, 128, "wbs%d" % t, t)
         for b in range(4):
             for k in range(2):
-                act(R("e2x", 128 * b + 64 * k, 128 * b + 64 * k + 64), R("xs", PT * b + 1, PT * b + 65), F.Copy, scale=0.5)
+                act(R("e2x", 128 * b + 64 * k, 128 * b + 64 * k + 64), R("xs", PT * b, PT * b + 64), F.Copy, scale=0.5)
         if t == 0:
             for b in range(4):
                 quant(R("qe%d" % b), R("se%d" % b), R("ex", 3 - b, 515 - b))
@@ -465,9 +474,9 @@ def rank_program(g, core, T, topo):
         if t == 0:
             later_constants()
         place(3)
-        ts(R("w3"), R("ck3"), col("km3"), A.is_equal)
         for n in (1, 2, 3):
             ts(col("af%d" % n), col("ao%d" % n), 1.0, A.add)
+            ts(R("w%d" % n), R("ck%d" % n), col("km%d" % n), A.is_equal)
             tt(R("c%d" % n), R("w%d" % n), R("k16"), A.mult)
             red(col("cb%d" % n), R("c%d" % n), A.add)
         tt(col("cb4"), col("cb1"), col("cb2"), A.add)
@@ -500,8 +509,6 @@ def rank_program(g, core, T, topo):
         for b in range(4):
             tt(R(X2, b, 1024, 4), R("dwn", PD * b, PD * b + PD), R(X, b, 1024, 4), A.add, off=R("so"))
         quant(R("qx%d" % (t + 1)), R("sx%d" % (t + 1)), R(X2))
-        if t == 0:
-            planes(X2)
     mm(R("pr", 0, 256), R("qv"), R("sv"), R("qx2"), R("sx2"))
     dma("y", T.oc[:], ap(R("qx2")).bitcast(dt.uint8), (), [R("qx2")])
     for k in range(4):

from concourse.bass import DstId, RemoteDMATransfer
from concourse.mybir import dt, AluOpType as A, AxisListType, ActivationFunctionType as F

N = 8
BIG = float(2.0 ** 90)
PT = 336
NO = 320
PD = 272
WD = (128, 128, 192, 256)
SCRATCH = {}
PLACE = {}
PSUM = ("pr", "pd")


def _decl():
    f, b, i, h, q, s = "float32", "bfloat16", "int32", "uint16", "float8_e4m3fn_x4", "uint8"

    def add(names, n, d, where="sbuf"):
        for k in names.split():
            SCRATCH[k] = (where, [128, n], d)
            PLACE[k] = (k, 0, n)

    def share(buf, d, *groups):
        at = 0
        for names, n in groups:
            for k in names.split():
                PLACE[k] = (buf, at, n)
                at += -(-n // 32) * 32
        SCRATCH[buf] = ("sbuf", [128, at], d)
    add("pr pd", 2048, f, "psum")
    add("ub vb", 512, b)
    add("qu qv", 128, q), add("su sv", 128, s)
    add("qu2", 256, q), add("su2", 256, s)
    add("wq", 512, q), add("wsc", 512, s)
    share("ci", i, ("iD dl", 256), ("iC", 512), ("iL", 8), ("iP pq pc pg", 2), ("iS", 16))
    share("cfl", f, ("fI maskb d0 ones io20 kk01 bigt", 256), ("ek", 2056), ("tb", 264), ("cf ch ca1 ca2 ca3 kf kc0 pgf gpf", 2), ("s16p c16 k16", 16))
    add("ul", 16, h)
    add("gt", 512, b), add("hf ex", 516, b)
    share("qk", q, ("qg qe0 qe1 qe2 qe3", 128)), share("sk", s, ("sg se0 se1 se2 se3", 128))
    for k in range(4):
        add("cm%d" % k, 4 * WD[k], b)
    add("cme", 1024, b)
    share("qc", q, ("qc0 qc1", 128), ("qc2", 192), ("qc3 qce", 256)), share("sc", s, ("sc0 sc1", 128), ("sc2", 192), ("sc3 sce", 256))
    add("dd ow sg1 sg2 pay dw2 ow2 win cum dw3 ow3 ycp slr", 256, f), add("junk", 1920, b), add("junk2", 768, b)
    add("rl13 rl14 rl15", 256, b)
    share("sm", f, ("rs rt rk ck1 ck2 ck3 bs2 bs3 bt io w1 w2 w3 xa xb t1 t2 t3 en vl plf c1 c2 c3 z1 z2 z3 y1 y2 y3 sv1 rl sf", 16),
          ("tm ac1 ac2 ac3 km1 km2 km3 kx1 kx2 kcb kcc fr1 fr2 fr3 dda em af1 af2 af3 cb1 cb2 cb3 cb4 db2 db3 db4 da2 da3 e1 e2", 2))
    share("li", h, ("ro pl so ol", 16), ("ky1 ky2 ky3 ao1 ao2 ao3", 2))
    add("xp", 1024, b), add("xs", 4 * PT, b), add("e2x", 512, b), add("dwn", 4 * PD, b)
    add("b13 b02 za zb ha hb", 512, b), add("qza qzb", 128, q), add("sza szb", 128, s)
    for t in range(3):
        add("xi%d" % t, 1024, b), add("qx%d" % t, 256, q), add("sx%d" % t, 256, s)
    for t in range(2):
        add("qb%d lbc%d lhc%d qh%d" % ((t,) * 4), 128, q)
        add("sb%d lbs%d lhs%d sh%d" % ((t,) * 4), 128, s)
        add("wbc%d whc%d" % (t, t), 192, q), add("wbs%d whs%d" % (t, t), 192, s)
        add("rbc%d rhc%d" % (t, t), 64, q), add("rbs%d rhs%d" % (t, t), 64, s)


_decl()
SEMAPHORES = ["ev", "es", "et", "eg", "loc"] + ["d%d" % k for k in range(14)] + [
    "%s%s%d" % (a, b, t) for a in ("rc", "rs", "ao", "ad") for b in "bh" for t in range(2)]


def _relays(topo, cores, r):
    c = cores[r]
    own = [d for d in topo.cores_of(c) if d != c and topo.may_write(d, cores[(r + 1) % N]) and topo.may_write(d, cores[(r + 3) % N])]
    near, far = [[d for d in own if (topo.die(d) == topo.die(c)) == same] for same in (True, False)]
    return [(near[0], "c", 0), (near[-1], "s", 0), (far[0], "c", 1), (far[-1], "s", 1)]


def _mask(engines):
    return sum(1 << int(e) for e in engines)


def _relay(g, core, T, topo, r, w, i):
    n = 0
    for t in range(2):
        for ph in "bh":
            k = 2 * i + 1
            dst = T.cores[(r + (k if ph == "b" else -k)) % N]
            rid, pid = topo.addr(dst, core)
            en = topo.engines(core, dst)
            g.wait_ge(T.sem["r%s%s%d" % (w, ph, t)], 8)
            src, d = T["r%s%s%d" % (ph, w, t)][:, 0:64], T["l%s%s%d" % (ph, w, t)][:, 64 * i:64 * i + 64]
            if w == "c":
                src, d = src.bitcast(dt.uint8), d.bitcast(dt.uint8)
            g.remote_dma(out_ap=d, in_ap=src, remote_sem=T.sem["ao%s%d" % (ph, t)], local_sem=T.sem.loc, pid=pid, routing_id=rid,
                         dma_engine_mask=_mask(en))
            n += len(en)
    g.wait_ge(T.sem.loc, n)


def rank_program(g, core, T, topo):
    rank = T.rank_of(core)
    if rank is None:
        for r in range(N):
            if core in topo.cores_of(T.cores[r]):
                for d, w, i in _relays(topo, T.cores, r):
                    if d == core:
                        _relay(g, core, T, topo, r, w, i)
        return
    eng = {"v": g.vector, "s": g.scalar, "t": g.tensor, "g": g, "y": g.sync}
    seen = {q: {} for q in eng}
    tot, snap, acc, nd = {}, {}, {}, [0]

    def R(n, lo=0, hi=None, st=1):
        buf, at, w = PLACE[n]
        return (buf, at + lo, at + (w if hi is None else hi), st)

    def ap(r):
        n, lo, hi, st = r
        return T[n][:, lo:hi] if st == 1 else T[n][:, lo:hi:st]

    def meet(a, b):
        if a[0] in PSUM:
            return a[1] // 512 <= (b[2] - 1) // 512 and b[1] // 512 <= (a[2] - 1) // 512
        if a[1] >= b[2] or b[1] >= a[2]:
            return False
        return not (a[3] == b[3] and a[3] > 1 and (a[1] - b[1]) % a[3])

    def wait(q, sem, val):
        if seen[q].get(sem, 0) >= val:
            return
        eng[q].wait_ge(T.sem[sem], val)
        seen[q][sem] = val
        for k, v in snap.get((sem, val), {}).items():
            seen[q][k] = max(seen[q].get(k, 0), v)

    def before(q, outs, ins, own, open_=False):
        need = {}
        for r, wr in [(r, True) for r in outs] + [(r, False) for r in ins]:
            for o, ow, sem, val, oq in acc.get(r[0], ()):
                if not (wr or ow or (r[0] in PSUM and oq != own)) or not meet(r, o):
                    continue
                if oq == own == "t" and open_:
                    continue
                need[sem] = max(need.get(sem, 0), val)
        for sem in sorted(need):
            wait(q, sem, need[sem])

    def after(q, outs, ins, sem, val, own):
        snap[(sem, val)] = dict(seen[q])
        for r in outs:
            l = acc.setdefault(r[0], [])
            if r[3] == 1 and r[0] not in PSUM:
                l[:] = [e for e in l if not (e[0][1] >= r[1] and e[0][2] <= r[2])]
            l.append((r, True, sem, val, own))
        for r in ins:
            acc.setdefault(r[0], []).append((r, False, sem, val, own))

    def op(q, outs, ins, call, open_=False):
        before(q, outs, ins, q, open_)
        sem = "e" + q
        tot[sem] = tot.get(sem, 0) + 1
        call(eng[q]).then_inc(T.sem[sem], 1)
        after(q, outs, ins, sem, tot[sem], q)

    def dma(q, out, in_, outs=(), ins=()):
        before(q, outs, ins, "dma")
        sem = "d%d" % nd[0]
        nd[0] += 1
        tot[sem] = 16
        eng[q].dma_start(out, in_).then_inc(T.sem[sem], 16)
        after(q, outs, ins, sem, 16, "dma")

    def lands(sem, val, regions):
        tot[sem] = val
        after("g", regions, (), sem, val, "remote")
        snap[(sem, val)] = {}

    def ts(out, i, s1, op0, s2=None, op1=None, off=None):
        cols = [s for s in (s1, s2) if isinstance(s, tuple)]
        a1 = ap(s1) if isinstance(s1, tuple) else s1
        a2 = ap(s2) if isinstance(s2, tuple) else s2
        src = ap(i) if off is None else ap(i).indirect(ap(off))
        kw = {} if op1 is None else {"op1": op1}
        op("v", [out], [i] + cols + ([off] if off else []),
           lambda e: e.tensor_scalar(out=ap(out), in0=src, scalar1=a1, scalar2=a2, op0=op0, **kw))

    def tt(out, a, b, o, off=None):
        src = ap(a) if off is None else ap(a).indirect(ap(off))
        op("v", [out], [a, b] + ([off] if off else []), lambda e: e.tensor_tensor(out=ap(out), in0=src, in1=ap(b), op=o))

    def cp(out, i, off=None, scatter=None):
        src = ap(i) if off is None else ap(i).indirect(ap(off))
        dst = ap(out) if scatter is None else ap(out).indirect(ap(scatter))
        op("v", [out], [i] + [o for o in (off, scatter) if o], lambda e: e.tensor_copy(out=dst, in_=src))

    def scan(out, a, b, o0, o1):
        op("v", [out], [a, b], lambda e: e.tensor_tensor_scan(out=ap(out), data0=ap(a), data1=ap(b), initial=0.0, op0=o0, op1=o1))

    def red(out, i, o):
        op("v", [out], [i], lambda e: e.tensor_reduce(out=ap(out), in_=ap(i), axis=AxisListType.X, op=o))

    def fill(out, c):
        op("v", [out], [], lambda e: e.memset(ap(out), c))

    def act(out, i, fn, bias=None, scale=None, accum=None, off=None):
        src = ap(i) if off is None else ap(i).indirect(ap(off))
        kw = {}
        if bias is not None:
            kw["bias"] = ap(bias) if isinstance(bias, tuple) else bias
        if scale is not None:
            kw["scale"] = scale
        if accum is not None:
            kw["accum_out"] = ap(accum)
        op("s", [out] + ([accum] if accum else []), [i] + [o for o in (bias, off) if isinstance(o, tuple)],
           lambda e: e.activation(out=ap(out), in_=src, func=fn, **kw))

    def quant(q, s, i):
        op("v", [q, s], [i], lambda e: e.quantize_mx(ap(q), ap(s), ap(i)))

    def mm(out, l, ls, r, rs, start=True, stop=True):
        op("t", [out], [l, ls, r, rs], lambda e: e.matmul_mx(ap(out), ap(l), ap(ls), ap(r), ap(rs), start, stop), not start)

    def iota(out, pattern, base, cm, flag=False):
        kw = {"allow_small_or_imprecise_dtypes": True} if flag else {}
        op("g", [out], [], lambda e: e.iota(ap(out), pattern, base, cm, **kw))

    def select(out, i, pattern, cmp, c, base, cm):
        op("g", [out], [i], lambda e: e.affine_select(ap(out), ap(i), pattern, cmp, c, base, cm))

    def col(n):
        return R(n, 0, 1)

    def planes(x):
        for b in range(4):
            act(R("xp", 256 * b, 256 * b + 256), R(x, b, 1024, 4), F.Copy)

    dma("y", ap(R("xi0")), T.x[:], [R("xi0")])
    dma("s", ap(R("ub")), T.u[:], [R("ub")])
    dma("y", ap(R("wq")).bitcast(dt.uint8), T.wc[:], [R("wq")])
    dma("y", ap(R("wsc")), T.ws[:], [R("wsc")])
    dma("y", ap(R("vb")), T.v[:], [R("vb")])
    iota(R("iP"), [[0, 2]], 0, 1)
    iota(R("iL"), [[16, 8]], 0, 0)
    iota(R("fI"), [[1, 256]], 0, 0, True)
    iota(R("iD"), [[0, 16], [1, 16]], 128, -1)
    act(R("bigt"), R("fI"), F.Identity, bias=BIG, scale=0.0)
    for b in (1, 2, 3):
        act(R("cme", b, 1024, 4), R("fI"), F.Copy, scale=0.0)
    iota(R("iC"), [[1, 8], [0, 64]], 0, 0)
    select(R("d0"), R("bigt"), [[0, 16], [1, 16]], A.is_equal, -BIG, 0, 0)
    iota(R("c16"), [[16, 16]], -1, 0, True)
    iota(R("ek"), [[1, 2056]], 0, 0, True)
    iota(R("iS"), [[0, 4], [16, 4]], 0, 1)
    iota(R("k16"), [[16, 4], [0, 4]], 0, 0, True)
    for c, k in enumerate((1, 3, 2, 0)):
        iota(R("tb", 64 * c, 64 * c + 64), [[1, 64]], 64 * k, 0, True)
    for a in range(4):
        fill(R("cm%d" % a, 4 * 16 * (4 * a + 1), 4 * WD[a]), 0.0)
    fill(R("rs", 0, 1), 0.0)
    ts(R("pq"), R("iP"), 15, A.bitwise_and)
    ts(R("pc"), R("pq"), 2, A.arith_shift_right)
    cp(R("cf"), R("pc"))
    ts(R("ch"), R("cf"), 2.0, A.is_ge)
    ts(R("ca1"), R("cf"), 2.0, A.mult, 1.0, A.add)
    ts(R("ca2"), R("cf"), 4.0, A.mult, -5.0, A.add)
    tt(R("ca3"), R("ca2"), R("ch"), A.mult)
    tt(R("kf"), R("ca1"), R("ca3"), A.subtract)
    ts(R("ul", 0, 8), R("iL"), 4.0, A.add)
    ts(R("ul", 8, 16), R("iL"), col("kf"), A.add)
    ts(R("dl"), R("iD"), 15, A.bitwise_and)
    ts(R("kk01"), R("dl"), 0.0, A.is_gt, 2.0 * BIG, A.mult)
    act(R("maskb"), R("kk01"), F.Identity, bias=-BIG)
    ts(R("pg"), R("iP"), 4, A.arith_shift_right)
    cp(R("gpf"), R("pg"))
    quant(R("qu"), R("su"), R("ub"))
    op("v", [R("qu2")], [R("qu"), R("ul")],
       lambda e: e.tensor_copy(ap(R("qu2")).bitcast(dt.uint32), ap(R("qu")).bitcast(dt.uint32).indirect(ap(R("ul")))))
    act(R("su2"), R("su"), F.Copy, off=R("ul"))
    act(R("io20"), R("fI"), F.Copy, scale=2.0 ** -20)
    act(R("ones"), R("fI"), F.Identity, bias=1.0, scale=0.0)
    quant(R("qx0"), R("sx0"), R("xi0"))
    ts(R("gt"), R("iC"), col("gpf"), A.is_equal)
    quant(R("qg"), R("sg"), R("gt"))

    def late_constants():
        ts(R("kc0"), R("kf"), -1.0, A.mult, 1027.0, A.add)
        ts(R("pgf"), R("gpf"), 16.0, A.mult)
        ts(R("s16p"), R("iS"), col("pgf"), A.subtract, -float(NO), A.add)
        for b in range(4):
            fill(R("xs", PT * b + 256, PT * b + PT), 0.0)
        fill(R("hf"), 0.5)
        select(R("ex"), R("hf"), [[-1, 516]], A.is_equal, 0.0, 3, 4)

    def later_constants():
        for b in range(4):
            fill(R("dwn", PD * b + 256, PD * b + PD), 0.0)
        fill(R("tb", 256, 264), -1.0)
        quant(R("qv"), R("sv"), R("vb"))

    rel = {(w, i): d for d, w, i in _relays(topo, T.cores, rank)}
    nloc = [0]

    def view(n, a, b, w):
        v = T[n][:, a:b]
        return v.bitcast(dt.uint8) if w == "c" else v

    def send_two(ph, w, src, t):
        before("g", (), [R(src)], "remote")
        tr = []
        for i in range(2):
            rid, pid = topo.addr(rel[(w, i)], core)
            en = topo.engines(core, rel[(w, i)])
            h = len(en) // 2
            en = en[i * h:i * h + h]
            tr.append(RemoteDMATransfer(dst_ids=[DstId(rid=rid, pnc=pid)], dma_engine_mask=_mask(en), remote_sem=T.sem["r%s%s%d" % (w, ph, t)],
                                        src=view(src, 64 * i, 64 * i + 64, w), dst=view("r%s%s%d" % (ph, w, t), 0, 64, w)))
            nloc[0] += h
        g.remote_dma_fused(tr, local_sem=T.sem.loc)

    def send_one(ph, w, src, a, dst, to, land, t):
        before("g", (), [R(src, a, a + 64)], "remote")
        rid, pid = topo.addr(dst, core)
        en = topo.engines(core, dst)
        g.remote_dma(out_ap=view(land, to, to + 64, w), in_ap=view(src, a, a + 64, w), remote_sem=T.sem["ad%s%d" % (ph, t)],
                     local_sem=T.sem.loc, pid=pid, routing_id=rid, dma_engine_mask=_mask(en))
        nloc[0] += len(en)

    def layer(qb, sb, off, z, qz, sz, h, qh, sh, hoff):
        for b in range(4):
            mm(R("pd", 512 * b, 512 * b + 128), R("qe%d" % b), R("se%d" % b), R(qb, off, off + 128), R(sb, off, off + 128))
        for b in range(4):
            tt(R(z, b, 512, 4), R("pd", 512 * b, 512 * b + 128), R("e2x", 128 * b, 128 * b + 128), A.add)
        quant(R(qz), R(sz), R(z))
        for b in (2, 0, 3, 1):
            mm(R("pr", 512 * b, 512 * b + 128), R("wq", 128 * b, 128 * b + 128), R("wsc", 128 * b, 128 * b + 128), R(qz), R(sz))
        for b in (2, 0, 3, 1):
            o, i = R(h, b, 512, 4), R("pr", 512 * b, 512 * b + 128)
            if b < 2:
                ts(o, i, 0.03125, A.mult)
            else:
                act(o, i, F.Copy, scale=0.03125)
        quant(R(qh, hoff, hoff + 128), R(sh, hoff, hoff + 128), R(h))

    def unpack(q, s, off, to):
        for b in (2, 0, 3, 1):
            mm(R("pd", 512 * b, 512 * b + 128), R("qe%d" % b), R("se%d" % b), R(q, off, off + 128), R(s, off, off + 128))
        for b in (2, 0, 3, 1):
            o, i = R("dwn", PD * b + to, PD * b + to + 128), R("pd", 512 * b, 512 * b + 128)
            if b < 2:
                ts(o, i, 2.0, A.mult)
            else:
                act(o, i, F.Copy, scale=2.0)

    def count(n, m, bias):
        act(R("junk2", 256 * n - 256, 256 * n), R("cum"), F.Sign, bias=bias, scale=-float(m), accum=col("ac%d" % n))

    def answer(n, kc):
        ts(col("ky%d" % n), col("ac%d" % n), -4.0, A.mult, col(kc), A.add)
        cp(R("ck%d" % n), R("ek"), off=col("ky%d" % n))
        red(col("km%d" % n), R("ck%d" % n), A.max)

    def edge(n):
        act(col("fr%d" % n), col("km%d" % n), F.Identity, bias=257.375, scale=-0.125)
        act(col("e%d" % n), col("km%d" % n), F.Identity, bias=256.875 - NO, scale=-0.125)

    def place(n):
        ts(col("ao%d" % n), col("km%d" % n), -0.125, A.mult, 256.375, A.add)

    for t in range(2):
        X, Q, S = "xi%d" % t, "qx%d" % t, "sx%d" % t
        pa, pv, pc = R("pr", 0, 256), R("pr", 512, 768), R("pr", 1024, 1280)
        mm(pa, R("qu2", 0, 128), R("su2", 0, 128), R(Q), R(S))
        mm(pv, R("qu2", 128, 256), R("su2", 128, 256), R(Q), R(S))
        mm(R("pr", 1536, 1792), R("qu2", 0, 128), R("su2", 0, 128), R(Q), R(S))
        act(R("sg1"), pv, F.Sign)
        act(R("sg2"), R("sg1"), F.Relu)
        tt(R("dd"), pa, R("maskb"), A.max)
        scan(R("ow"), R("d0"), R("dd"), A.max, A.min)
        share = (15, 14) if t == 0 else (15, 14, 13)
        for m in share:
            own, e, n = R("ow", 16 * m + 15, 16 * m + 16), m - 12, 16 * m
            act(R("rl%d" % m, 0, n + 16), R("pr", 1536, 1552 + n), F.Relu, bias=own, scale=-1.0)
            act(R("cm3", e, 4 * n, 4), R("rl%d" % m, 0, n), F.Sign, accum=R("rs", m, m + 1))
            act(R("cm3", 4 * n + e, 4 * n + 64, 4), R("rl%d" % m, n, n + 16), F.Sign)
        tt(R("cme", 0, 1024, 4), pa, R("ow"), A.is_equal)
        quant(R("qce"), R("sce"), R("cme"))
        mm(pc, R("qg"), R("sg"), R("qce"), R("sce"), True, False)
        for m in (13, 12, 11, 10, 9, 8, "q2", 7, 6, 5, 4, "q1", "q3", 3, 2, 1, 0, "q0"):
            if m in share:
                continue
            if isinstance(m, int):
                a, e = m // 4, m % 4
                ts(R("cm%d" % a, e, 64 * m + 64, 4), R("pr", 0, 16 * m + 16), R("ow", 16 * m + 15, 16 * m + 16), A.is_lt)
                if m:
                    act(R("junk", 8 * m * (m - 1), 8 * m * (m + 1)), R("cm%d" % a, e, 64 * m, 4), F.Copy, accum=R("rs", m, m + 1))
            else:
                a = int(m[1])
                quant(R("qc%d" % a), R("sc%d" % a), R("cm%d" % a))
                mm(R("pr", 1024, 1024 + WD[a]), R("qg"), R("sg"), R("qc%d" % a), R("sc%d" % a), False, a == 0)
        planes(X)
        tt(R("pay"), R("sg2"), R("io20"), A.add)
        tt(R("rt"), R("rs"), R("c16"), A.subtract)
        tt(R("dw2"), pc, R("maskb"), A.max)
        scan(R("ow2"), R("d0"), R("dw2"), A.max, A.min)
        tt(R("rk"), R("ow2", 15, 256, 16), R("rt"), A.subtract)
        cp(R("ro"), R("rk"))
        cp(R("win"), R("pay"), scatter=R("ro"))
        scan(R("cum"), R("win"), R("ones"), A.add, A.add)
        ts(col("tm"), R("cum", 255, 256), -0.5, A.add)
        count(1, 4, col("tm"))
        if t == 0:
            late_constants()
        tt(R("dw3"), R("win"), R("maskb"), A.max)
        answer(1, "kc0")
        edge(1)
        place(1)
        ts(R("bs2"), R("cum"), 2.0, A.mult, col("tm"), A.add, off=col("ao1"))
        count(2, 3, R("bs2", 0, 1))
        ts(col("kx1"), col("ky1"), col("km1"), A.is_equal, -5000.0, A.mult)
        tt(col("kcb"), col("kx1"), col("kc0"), A.add)
        scan(R("ow3"), R("d0"), R("dw3"), A.max, A.min)
        answer(2, "kcb")
        edge(2)
        place(2)
        ts(R("bs3"), R("cum"), 1.0, A.mult, col("tm"), A.add, off=col("ao2"))
        count(3, 2, R("bs3", 0, 1))
        ts(R("bt"), R("ow3", 15, 256, 16), 1.0, A.is_ge)
        ts(col("kx2"), col("ky2"), col("km2"), A.is_equal, -5000.0, A.mult)
        tt(R("io"), R("ow3", 15, 256, 16), R("bt"), A.subtract)
        tt(col("kcc"), col("kx2"), col("kcb"), A.add)
        ts(R("ol"), R("io"), 2.0 ** 20, A.mult)
        for b in range(4):
            act(R("xs", PT * b, PT * b + 256), R("xp", 256 * b, 256 * b + 256), F.Copy, off=R("ol"))
        ts(R("t1"), R("ck2"), col("km2"), A.is_equal, col("fr1"), A.mult)
        ts(R("xa"), R("ck1"), col("km1"), A.is_equal, col("e1"), A.mult)
        ts(R("xb"), R("ck2"), col("km2"), A.is_equal, col("e2"), A.mult)
        tt(R("t1"), R("t1"), R("s16p"), A.add)
        tt(R("xa"), R("xa"), R("xb"), A.add)
        answer(3, "kcc")
        ts(col("fr3"), col("km3"), -0.125, A.mult, 257.375, A.add)
        ts(col("em"), col("km3"), -0.125, A.mult, 256.875 - NO, A.add)
        ts(col("dda"), col("fr3"), -1.0, A.mult, col("fr2"), A.add)
        ts(R("t3"), R("ck3"), 0.0, A.is_gt, col("fr3"), A.mult)
        ts(R("en"), R("ck3"), col("km3"), A.is_equal, col("em"), A.mult)
        ts(R("t2"), R("ck3"), col("km3"), A.is_equal, col("dda"), A.mult)
        tt(R("t1"), R("t1"), R("t3"), A.add)
        tt(R("en"), R("en"), R("xa"), A.add)
        tt(R("t1"), R("t1"), R("t2"), A.add)
        tt(R("vl"), R("t1"), R("en"), A.is_lt)
        tt(R("plf"), R("t1"), R("vl"), A.mult)
        ts(R("pl"), R("plf"), float(NO), A.add)
        for o, lo, q, s in (("b13", 0, "qb%d" % t, "sb%d" % t), ("b02", 8, "wbc%d" % t, "wbs%d" % t)):
            for b in (2, 0, 3, 1):
                if b < 2:
                    cp(R(o, b, 512, 4), R("xs", PT * b, PT * b + PT), off=R("pl", lo, lo + 8))
                else:
                    act(R(o, b, 512, 4), R("xs", PT * b, PT * b + PT), F.Copy, off=R("pl", lo, lo + 8))
            quant(R(q, 0, 128), R(s, 0, 128), R(o))
            if lo == 0:
                send_two("b", "c", q, t)
                send_two("b", "s", s, t)
        d2 = T.cores[(rank + 2) % N]
        send_one("b", "c", "wbc%d" % t, 0, d2, 128, "wbc%d" % t, t)
        send_one("b", "s", "wbs%d" % t, 0, d2, 128, "wbs%d" % t, t)
        for b in range(4):
            for k in range(2):
                act(R("e2x", 128 * b + 64 * k, 128 * b + 64 * k + 64), R("xs", PT * b, PT * b + 64), F.Copy, scale=0.5)
        if t == 0:
            for b in range(4):
                quant(R("qe%d" % b), R("se%d" % b), R("ex", 3 - b, 515 - b))
        lands("adb%d" % t, 16, [R("wbc%d" % t, 128, 192), R("wbs%d" % t, 128, 192)])
        lands("aob%d" % t, 32, [R("lbc%d" % t), R("lbs%d" % t)])
        layer("wbc%d" % t, "wbs%d" % t, 64, "za", "qza", "sza", "ha", "whc%d" % t, "whs%d" % t, 64)
        p2 = T.cores[(rank - 2) % N]
        send_one("h", "c", "whc%d" % t, 128, p2, 0, "whc%d" % t, t)
        send_one("h", "s", "whs%d" % t, 128, p2, 0, "whs%d" % t, t)
        layer("lbc%d" % t, "lbs%d" % t, 0, "zb", "qzb", "szb", "hb", "qh%d" % t, "sh%d" % t, 0)
        send_two("h", "c", "qh%d" % t, t)
        send_two("h", "s", "sh%d" % t, t)
        if t == 0:
            later_constants()
        place(3)
        for n in (1, 2, 3):
            ts(col("af%d" % n), col("ao%d" % n), 1.0, A.add)
            ts(R("w%d" % n), R("ck%d" % n), col("km%d" % n), A.is_equal)
            tt(R("c%d" % n), R("w%d" % n), R("k16"), A.mult)
            red(col("cb%d" % n), R("c%d" % n), A.add)
        tt(col("cb4"), col("cb1"), col("cb2"), A.add)
        tt(col("cb4"), col("cb4"), col("cb3"), A.add)
        ts(col("cb4"), col("cb4"), -1.0, A.mult, 384.0, A.add)
        for n in (2, 3, 4):
            tt(col("db%d" % n), col("cb%d" % n), col("cb%d" % (n - 1)), A.subtract)
        tt(col("da2"), col("af2"), col("af1"), A.subtract)
        tt(col("da3"), col("af3"), col("af2"), A.subtract)
        for n, d in ((1, "af1"), (2, "da2"), (3, "da3")):
            ts(R("y%d" % n), R("rk"), col("af%d" % n), A.is_ge, col(d), A.mult)
            ts(R("z%d" % n), R("rk"), col("af%d" % n), A.is_ge, col("db%d" % (n + 1)), A.mult)
        tt(R("rl"), R("rk"), R("y1"), A.subtract)
        tt(R("rl"), R("rl"), R("y2"), A.subtract)
        tt(R("rl"), R("rl"), R("y3"), A.subtract)
        ts(R("sv1"), R("rl"), col("cb1"), A.add, -256.0, A.add)
        for n in (1, 2, 3):
            tt(R("sv1"), R("sv1"), R("z%d" % n), A.add)
        ts(R("vl"), R("rl"), 64.0, A.is_lt)
        tt(R("sf"), R("sv1"), R("vl"), A.mult)
        ts(R("so"), R("sf"), 256.0, A.add)
        if t == 1:
            act(R("slr"), R("tb"), F.Copy, off=R("so"))
            dma("y", T.sl[:], T.slr[0:128:16, :], (), [R("slr")])
        lands("adh%d" % t, 16, [R("whc%d" % t, 0, 64), R("whs%d" % t, 0, 64)])
        lands("aoh%d" % t, 32, [R("lhc%d" % t), R("lhs%d" % t)])
        unpack("whc%d" % t, "whs%d" % t, 0, 128)
        unpack("lhc%d" % t, "lhs%d" % t, 0, 0)
        X2 = "xi%d" % (t + 1)
        for b in range(4):
            tt(R(X2, b, 1024, 4), R("dwn", PD * b, PD * b + PD), R(X, b, 1024, 4), A.add, off=R("so"))
        quant(R("qx%d" % (t + 1)), R("sx%d" % (t + 1)), R(X2))
    mm(R("pr", 0, 256), R("qv"), R("sv"), R("qx2"), R("sx2"))
    dma("y", T.oc[:], ap(R("qx2")).bitcast(dt.uint8), (), [R("qx2")])
    for k in range(4):
        dma("s" if k % 2 else "y", T.osc[4 * k:4 * k + 4, :], T.sx2[32 * k:32 * k + 4, :], (), [R("sx2")])
    act(R("ycp"), R("pr", 0, 256), F.Copy)
    dma("s", T.y[:], ap(R("ycp")), (), [R("ycp")])
    tot["loc"] = nloc[0]
    for sem in sorted(tot):
        wait("g", sem, tot[sem])
